import numpy as np
import ml_dtypes


def mxq(x, axis, fmt="e4m3"):
    dtype, down = {"e4m3": (ml_dtypes.float8_e4m3fn, 7), "e5m2": (ml_dtypes.float8_e5m2, 14)}[fmt]
    v = np.moveaxis(np.asarray(x, np.float32).astype(ml_dtypes.bfloat16).astype(np.float64), axis, -1)
    blocks = v.reshape(v.shape[:-1] + (-1, 32))
    amax = np.abs(blocks).max(-1, keepdims=True)
    byte = np.maximum(np.where(amax > 0, np.frexp(amax)[1] - 1 + 127, 0) - down, 1)
    scale = np.exp2(byte - 127.0)
    codes = (blocks / scale).astype(np.float32).astype(dtype).astype(np.float64)
    return np.moveaxis((codes * scale).reshape(v.shape), -1, axis)


WIDE = False


def mx_kscale(k):
    if not WIDE:
        return np.ones(k)
    levels = np.array([10, -10, 5, -5, 0])
    if k % 512:
        return np.exp2(np.random.permutation(np.resize(levels, k // 32))).repeat(32)
    a = np.empty((k // 512, 16))
    for p in range(k // 512):
        a[p, :8] = np.random.permutation(np.resize(levels, 8))
        for g in range(8):
            far = levels[np.abs(levels - a[p, g]) >= 10]
            a[p, g + 8] = far[np.random.randint(len(far))]
    return np.exp2(a.ravel()).repeat(32)


BF16 = ml_dtypes.bfloat16


def bf(x):
    return np.asarray(x, np.float32).astype(BF16)


def f64(x):
    return np.asarray(x).astype(np.float64)


E2M1 = np.array([0.0, 0.5, 1.0, 1.5, 2.0, 3.0, 4.0, 6.0, -0.0, -0.5, -1.0, -1.5, -2.0, -3.0, -4.0, -6.0])


def pack_weight(w, fmt):
    k, n = w.shape
    w = f64(bf(w)).reshape(k // 32, 32, n)
    amax = np.abs(w).max(1)
    if fmt == "e4m3":
        byte = np.frexp(amax)[1] - 1 + 127 - 7
    else:
        mant, ex = np.frexp(amax / 6.0)
        byte = np.where(mant > 0.5, ex, ex - 1) + 127
    byte = np.clip(np.where(amax > 0, byte, 1), 1, 254)
    scaled = (w * np.exp2(127.0 - byte)[:, None, :]).reshape(k, n).astype(np.float32)
    by_word = np.ascontiguousarray(scaled.reshape(k // 512, 128, 4, n).transpose(0, 1, 3, 2))
    if fmt == "e4m3":
        words = by_word.astype(ml_dtypes.float8_e4m3fn).view(np.uint8)
    else:
        c = by_word.astype(ml_dtypes.float4_e2m1fn).view(np.uint8) & 0xF
        words = c[..., 0::2] | (c[..., 1::2] << 4)
    return np.ascontiguousarray(words), np.ascontiguousarray(byte.astype(np.uint8).reshape(k // 512, 16, n))


def unpack_weight(words, scales, fmt):
    g, p, n, _ = words.shape
    if fmt == "e4m3":
        vals = np.ascontiguousarray(words).view(ml_dtypes.float8_e4m3fn).astype(np.float64)
    else:
        nib = np.empty((g, p, n, 4), np.uint8)
        nib[..., 0::2] = words & 0xF
        nib[..., 1::2] = words >> 4
        vals = E2M1[nib]
    vals = vals * np.repeat(np.exp2(scales.astype(np.float64) - 127.0), 8, axis=1)[..., None]
    return vals.transpose(0, 1, 3, 2).reshape(g * 512, n)

E4M3FN = np.array([(-1.0 if i & 128 else 1.0) * ((1.0 + (i & 7) / 8.0) * 2.0 ** (((i >> 3) & 15) - 7) if i & 120 else (i & 7) * 2.0 ** -9) for i in range(256)])


def e4m3fn_bytes(y):
    return np.clip(np.asarray(y, np.float64), -448.0, 448.0).astype(np.float32).astype(ml_dtypes.float8_e4m3fn).view(np.uint8)


def e4m3fn_values(b):
    return E4M3FN[b]


N, F, D, E = 1024, 1024, 1024, 1024


def sigmoid(z):
    return 1.0 / (1.0 + np.exp(-z))


def draw0():
    s = mx_kscale(F)
    r = mx_kscale(N)
    t = np.random.standard_normal((N, F)) * s
    h = np.random.standard_normal((N, F)) * s
    v = np.random.standard_normal((F, D)) / np.sqrt(F) / s[:, None]
    v_words, v_scales = pack_weight(v, "e4m3")
    b = 0.3 * np.random.standard_normal(D)
    a = np.random.standard_normal((N, D))
    x = np.random.standard_normal((N, E)) / r[:, None]
    c = (1.0 + 0.1 * np.random.standard_normal(N)) * r
    return {"t": bf(t), "h": bf(h), "v_words": v_words, "v_scales": v_scales, "b": bf(b), "a": bf(a), "x": bf(x), "c": bf(c)}


def core(t, h, v_words, v_scales, b, a, x, c):
    n_rows = x.shape[0]
    vq = unpack_weight(v_words, v_scales, "e4m3")
    gt = np.tanh((mxq(f64(t), 1, "e4m3") @ vq) + f64(b)[None, :])
    gh = np.tanh((mxq(f64(h), 1, "e4m3") @ vq) + f64(b)[None, :])
    e = gt - gh
    q = f64(c)[:, None] * sigmoid(f64(a)) * e
    xq = mxq(f64(x), 0, "e4m3")
    u = (xq.T @ mxq(q, 0, "e4m3")) / np.sqrt(n_rows)
    return u


def setup_inputs():
    drawn = draw0()
    full = np.asarray(drawn['x']).astype(np.float64)
    scale = (np.abs(full).reshape(1024, 8, 128).max(axis=(2,)) / 448.0).astype(np.float32)
    given = {}
    for key, value in drawn.items():
        if key == 'x':
            given['x_bytes'] = e4m3fn_bytes(full / np.repeat(scale.astype(np.float64), 128, axis=1))
            given['x_scale'] = scale
        else:
            given[key] = value
    return given


def reference(t, h, v_words, v_scales, b, a, x_bytes, x_scale, c):
    return core(t, h, v_words, v_scales, b, a, e4m3fn_values(x_bytes) * np.repeat(x_scale.astype(np.float64), 128, axis=1), c)

@@ -1,0 +1,331 @@
+from contextlib import ExitStack
+
+import concourse.mybir as mybir
+from concourse.masks import make_identity
+
+F32 = mybir.dt.float32
+BF16 = mybir.dt.bfloat16
+I32 = mybir.dt.int32
+U32 = mybir.dt.uint32
+U8 = mybir.dt.uint8
+FP8 = mybir.dt.float8_e4m3fn
+FP8X4 = mybir.dt.float8_e4m3fn_x4
+ACT = mybir.ActivationFunctionType
+ALU = mybir.AluOpType
+
+P = 128
+SIZE = 1024
+FLOPS = 3 * 2 * SIZE * SIZE * SIZE
+
+
+def tile_differencetargetpropweightstep_d1p_kernel(
+    tc, t, h, v_words, v_scales, b, a, x_bytes, x_scale, c, out
+):
+    nc = tc.nc
+    with ExitStack() as ctx:
+        const = ctx.enter_context(tc.tile_pool(name="const", bufs=1))
+        work = ctx.enter_context(tc.tile_pool(name="work", bufs=2))
+        psum = ctx.enter_context(tc.psum_pool(name="psum", bufs=2))
+        ctx.enter_context(tc.manual_schedule())
+
+        def keep(name, shape, dtype):
+            return const.tile(shape, dtype, name=name, align_bytes=64)
+
+        ident = keep("ident", [P, P], F32)
+        make_identity(nc, ident[:])
+        v_sc = keep("v_sc", [P, SIZE], U8)
+        nc.vector.memset(v_sc[:].bitcast(I32), 0)
+        b_rows = keep("b_rows", [P, P], BF16)
+        nc.vector.memset(b_rows[:], 0.0)
+        warm = keep("warm", [P, 2], F32)
+
+        def rows4(ap):
+            return ap.rearrange("(g p t) k -> g p t k", g=2, p=P, t=4)
+
+        raw = {}
+
+        def load_bf16(key, ap, g, parts):
+            tl = keep("raw_%s%d" % (key, g), [P, 4, SIZE], BF16)
+            raw[key, g] = tl
+            s = 0
+            for n in parts:
+                nc.sync.dma_start(out=tl[:, s : s + n, :], in_=rows4(ap)[g][:, s : s + n, :])
+                s += n
+
+        def load_cols(key, ap, g, half):
+            if half == 0:
+                raw[key, g] = keep("raw_%s%d" % (key, g), [P, 4, SIZE], BF16)
+            cols = slice(512 * half, 512 * (half + 1))
+            nc.sync.dma_start(out=raw[key, g][:, :, cols], in_=rows4(ap)[g][:, :, cols])
+
+        x_b = []
+
+        def load_x(g):
+            tl = keep("x_b%d" % g, [P, 4, SIZE], U8)
+            nc.sync.dma_start(out=tl[:], in_=rows4(x_bytes)[g])
+            x_b.append(tl)
+
+        load_bf16("t", t, 0, (1, 1, 2))
+        nc.scalar.activation(out=warm[:], in_=b_rows[:, 0:2], func=ACT.Sigmoid)
+        vs32 = v_scales.bitcast(I32)
+        for q in range(4):
+            nc.sync.dma_start(
+                out=v_sc[32 * q : 32 * q + 8, :].bitcast(I32),
+                in_=vs32[:, 4 * q : 4 * q + 4, :],
+            )
+        nc.scalar.dma_start(out=b_rows[0:8, :], in_=b.rearrange("(j p) -> j p", p=P))
+        c_bf = keep("c_bf", [P, 2, 4], BF16)
+        nc.scalar.dma_start(out=c_bf[:], in_=c.rearrange("(g p t) -> p g t", g=2, p=P, t=4))
+        x_sc = keep("x_sc", [P, 2, 32], F32)
+        nc.scalar.dma_start(out=x_sc[:], in_=x_scale.rearrange("(g p t) j -> p g (t j)", g=2, p=P, t=4))
+        load_bf16("h", h, 0, (2, 2))
+        v_w = []
+        for g in range(2):
+            tl = keep("v_w%d" % g, [P, SIZE], U32)
+            nc.sync.dma_start(out=tl[:].bitcast(I32), in_=v_words[g].rearrange("p n t -> p (n t)").bitcast(I32))
+            v_w.append(tl)
+        load_x(0)
+        load_cols("a", a, 0, 0)
+        load_bf16("t", t, 1, (4,))
+        load_cols("a", a, 0, 1)
+        load_bf16("h", h, 1, (4,))
+        load_x(1)
+        load_cols("a", a, 1, 0)
+        load_cols("a", a, 1, 1)
+
+        c32 = keep("c32", [P, 2, 4], F32)
+        b_f32 = keep("b_f32", [P, P], F32)
+        bias = keep("bias", [P, 8], F32)
+        nbias = keep("nbias", [P, 8], F32)
+
+        def small_vectors():
+            nc.vector.tensor_copy(out=c32[:], in_=c_bf[:])
+            nc.vector.tensor_copy(out=b_f32[:], in_=b_rows[:])
+            b_ps = psum.tile([P, 512], F32, name="b_ps", tag="m", bufs=4)
+            nc.tensor.transpose(b_ps[:, 0:P], b_f32[:], ident[:])
+            nc.vector.tensor_copy(out=bias[:], in_=b_ps[:, 0:8])
+            nc.vector.tensor_scalar(out=nbias[:], in0=b_ps[:, 0:8], scalar1=-1.0, scalar2=None, op0=ALU.mult)
+
+
+        grouped = {}
+        codes = {}
+        scales = {}
+
+        def turn_slot(key, g, s, tag, engine):
+            if s == 0:
+                grouped[key, g] = work.tile([P, 2, 512, 4], BF16, name="grouped", tag="grouped", bufs=3, align_bytes=64)
+            words = raw[key, g][:, s, :].bitcast(F32)
+            ps = psum.tile([P, 2, 2, P], F32, name="turn_ps", tag=tag, bufs=4)
+            for gk in range(2):
+                for u in range(2):
+                    nc.tensor.transpose(ps[:, gk, u, :], words[:, 256 * gk + u : 256 * (gk + 1) : 2], ident[:])
+            dst = grouped[key, g][:, :, P * s : P * (s + 1), :].rearrange("p k r f -> p k (r f)").bitcast(F32)
+            dst = dst.rearrange("p k (r u) -> p k r u", u=2)
+            src = ps[:].rearrange("p k u r -> p k r u")
+            if engine == "v":
+                nc.vector.tensor_copy(out=dst, in_=src)
+            else:
+                nc.scalar.copy(out=dst, in_=src)
+
+        def quantise_th(key, g, gk):
+            if gk == 0:
+                codes[key, g] = keep("codes_%s%d" % (key, g), [P, 2, 512], U32)
+                scales[key, g] = keep("scales_%s%d" % (key, g), [P, 2, 512], U8)
+            nc.vector.quantize_mx(
+                out=codes[key, g][:, gk, :].bitcast(FP8X4),
+                scales=scales[key, g][:, gk, :],
+                in_=grouped[key, g][:, gk, :, :].rearrange("p r f -> p (r f)"),
+            )
+
+        x_codes = {}
+        x_scales = {}
+        x_plane = {}
+        x_inter = {}
+
+        def x_widen(g, hf, s):
+            if s == 0:
+                x_plane[g, hf] = work.tile([P, 4, 512], BF16, name="x_plane", tag="x_plane")
+            for j in range(4):
+                cols = slice(512 * hf + P * j, 512 * hf + P * (j + 1))
+                nc.vector.tensor_scalar(
+                    out=x_plane[g, hf][:, s, P * j : P * (j + 1)],
+                    in0=x_b[g][:, s, cols].bitcast(FP8),
+                    scalar1=x_sc[:, g, 8 * s + 4 * hf + j : 8 * s + 4 * hf + j + 1],
+                    scalar2=None,
+                    op0=ALU.mult,
+                )
+
+        def x_interleave(g, hf):
+            x_inter[g, hf] = work.tile([P, 512, 4], BF16, name="x_inter", tag="x_inter", align_bytes=64)
+            nc.vector.tensor_copy(out=x_inter[g, hf][:], in_=x_plane[g, hf][:].rearrange("p s e -> p e s"))
+
+        def x_quantise(g, hf):
+            x_codes[g, hf] = keep("x_codes%d%d" % (g, hf), [P, 512], U32)
+            x_scales[g, hf] = keep("x_scales%d%d" % (g, hf), [P, 512], U8)
+            nc.vector.quantize_mx(
+                out=x_codes[g, hf][:].bitcast(FP8X4),
+                scales=x_scales[g, hf][:],
+                in_=x_inter[g, hf][:].rearrange("p e s -> p (e s)"),
+            )
+
+        x_work = []
+        chunks = [(g, hf) for g in range(2) for hf in range(2)]
+        for i in range(5):
+            for s in range(4):
+                if i < 4:
+                    x_work.append((x_widen, (*chunks[i], s)))
+                if i > 0 and s == 0:
+                    x_work.append((x_interleave, chunks[i - 1]))
+                if i > 0 and s == 1:
+                    x_work.append((x_quantise, chunks[i - 1]))
+
+        def do_x(n):
+            for fn, args in x_work[:n]:
+                fn(*args)
+            del_list = x_work[n:]
+            x_work.clear()
+            x_work.extend(del_list)
+
+        tanh_tiles = {}
+        sig = {}
+        weight = {}
+        e_ps = {}
+        q_in = {}
+        q_codes = {}
+        q_scales = {}
+
+        def forward(r, u, key):
+            g, dp = divmod(r, 4)
+            db = 2 * dp + u
+            z = psum.tile([P, 512], F32, name="z", tag="z", bufs=4)
+            for gk in range(2):
+                nc.tensor.matmul_mx(
+                    out=z[:],
+                    lhsT=v_w[gk][:, P * db : P * (db + 1)].bitcast(FP8X4),
+                    lhsT_scale=v_sc[4 * gk : P, P * db : P * (db + 1)],
+                    rhs=codes[key, g][:, gk, :].bitcast(FP8X4),
+                    rhs_scale=scales[key, g][:, gk, :],
+                    start=(gk == 0),
+                    stop=(gk == 1),
+                )
+            tl = work.tile([P, 512], F32, name="tanh_" + key, tag="tanh_" + key, bufs=5)
+            tanh_tiles[r, u, key] = tl
+            nc.scalar.activation(
+                out=tl[:],
+                in_=z[:],
+                func=ACT.Tanh,
+                bias=bias[:, db : db + 1] if key == "t" else nbias[:, db : db + 1],
+                scale=1.0 if key == "t" else -1.0,
+            )
+
+        def sigmoid(r):
+            g, dp = divmod(r, 4)
+            sig[r] = work.tile([P, 4, 256], F32, name="sig", tag="sig", bufs=2)
+            nc.scalar.activation(out=sig[r][:], in_=raw["a", g][:, :, 256 * dp : 256 * (dp + 1)], func=ACT.Sigmoid)
+
+        def row_weight(r):
+            g = r // 4
+            weight[r] = work.tile([P, 4, 256], F32, name="weight", tag="weight", bufs=2)
+            for s in range(4):
+                nc.vector.tensor_scalar(
+                    out=weight[r][:, s, :], in0=sig[r][:, s, :], scalar1=c32[:, g, s : s + 1], scalar2=None, op0=ALU.mult
+                )
+
+        def back(r):
+            for u in range(2):
+                ps = psum.tile([P, 4, P], F32, name="e_ps", tag="m", bufs=4)
+                e_ps[r, u] = ps
+                for s in range(4):
+                    for key in ("t", "h"):
+                        nc.tensor.matmul(
+                            ps[:, s, :],
+                            lhsT=tanh_tiles[r, u, key][:, P * s : P * (s + 1)],
+                            rhs=ident[:],
+                            is_transpose=True,
+                            start=(key == "t"),
+                            stop=(key == "h"),
+                        )
+
+        def error(r):
+            q_in[r] = work.tile([P, 256, 4], BF16, name="q_in", tag="q_in", align_bytes=64)
+            for u in range(2):
+                nc.vector.tensor_tensor(
+                    out=q_in[r][:, P * u : P * (u + 1), :],
+                    in0=e_ps[r, u][:].rearrange("p s d -> p d s"),
+                    in1=weight[r][:, :, P * u : P * (u + 1)].rearrange("p s d -> p d s"),
+                    op=ALU.mult,
+                )
+
+        def quantise_q(r):
+            q_codes[r] = keep("q_codes%d" % r, [P, 256], U32)
+            q_scales[r] = keep("q_scales%d" % r, [P, 256], U8)
+            nc.vector.quantize_mx(
+                out=q_codes[r][:].bitcast(FP8X4),
+                scales=q_scales[r][:],
+                in_=q_in[r][:].rearrange("p d s -> p (d s)"),
+            )
+
+        out_view = out.rearrange("(e p) d -> p e d", p=P)
+
+        def final(j):
+            for ep in range(4):
+                ps = psum.tile([P, 2, 256], F32, name="o_ps", tag="m", bufs=4)
+                for i in range(2):
+                    eb = 2 * ep + i
+                    hf, el = divmod(eb, 4)
+                    for g in range(2):
+                        nc.tensor.matmul_mx(
+                            out=ps[:, i, :],
+                            lhsT=x_codes[g, hf][:, P * el : P * (el + 1)].bitcast(FP8X4),
+                            lhsT_scale=x_scales[g, hf][:, P * el : P * (el + 1)],
+                            rhs=q_codes[4 * g + j][:].bitcast(FP8X4),
+                            rhs_scale=q_scales[4 * g + j][:],
+                            start=(g == 0),
+                            stop=(g == 1),
+                        )
+                res = work.tile([P, 2, 256], F32, name="res", tag="res", bufs=8)
+                if ep % 2 == 0:
+                    nc.scalar.activation(out=res[:], in_=ps[:], func=ACT.Copy, scale=1.0 / 32.0)
+                else:
+                    nc.vector.tensor_scalar(out=res[:], in0=ps[:], scalar1=1.0 / 32.0, scalar2=None, op0=ALU.mult)
+                nc.sync.dma_start(out=out_view[:, 2 * ep : 2 * ep + 2, 256 * j : 256 * (j + 1)], in_=res[:])
+
+        for s in range(4):
+            turn_slot("t", 0, s, "z", "vs"[s % 2])
+            if s == 1:
+                small_vectors()
+        for s in range(4):
+            turn_slot("h", 0, s, "m", "sv"[s % 2])
+            if s == 1:
+                quantise_th("t", 0, 0)
+            if s == 3:
+                quantise_th("t", 0, 1)
+        quantise_th("h", 0, 0)
+        quantise_th("h", 0, 1)
+        do_x(8)
+        late = [(key, s) for key in ("t", "h") for s in range(4)]
+        late_by_step = {1: late[0:3], 2: late[3:6], 3: late[6:8]}
+        for step in range(10):
+            if step < 8:
+                for key in ("t", "h"):
+                    for u in range(2):
+                        forward(step, u, key)
+                sigmoid(step)
+            if 1 <= step <= 8:
+                if step == 3:
+                    quantise_th("t", 1, 0)
+                    quantise_th("t", 1, 1)
+                row_weight(step - 1)
+                do_x(((0, 2,2,2,2,2) + (0,) * 9)[step])
+                back(step - 1)
+                error(step - 1)
+            for i, (key, s) in enumerate(late_by_step.get(step, [])):
+                turn_slot(key, 1, s, "m", "sss"[i])
+            if step == 3:
+                quantise_th("h", 1, 0)
+                quantise_th("h", 1, 1)
+            if 1 <= step <= 8:
+                quantise_q(step - 1)
+                do_x(((0, 2,2,2,2,2) + (0,) * 9)[step])
+            if step >= 6:
+                final(step - 6)

@@ -15,6 +15,8 @@ ALU = mybir.AluOpType
 
 P = 128
 SIZE = 1024
+SCALAR_WIDENS = ()
+GP_ROUNDS = (0, 1, 2, 3, 4, 5, 6, 7)
 FLOPS = 3 * 2 * SIZE * SIZE * SIZE
 
 
@@ -38,6 +40,8 @@ def tile_differencetargetpropweightstep_d1p_kernel(
         b_rows = keep("b_rows", [P, P], BF16)
         nc.vector.memset(b_rows[:], 0.0)
         warm = keep("warm", [P, 2], F32)
+        zeros = keep("zeros", [P, 512], BF16)
+        nc.vector.memset(zeros[:], 0.0)
 
         def rows4(ap):
             return ap.rearrange("(g p t) k -> g p t k", g=2, p=P, t=4)
@@ -66,7 +70,7 @@ def tile_differencetargetpropweightstep_d1p_kernel(
             x_b.append(tl)
 
         load_bf16("t", t, 0, (1, 1, 2))
-        nc.scalar.activation(out=warm[:], in_=b_rows[:, 0:2], func=ACT.Sigmoid)
+        nc.scalar.activation(out=warm[:], in_=zeros[:, 0:2], func=ACT.Sigmoid)
         vs32 = v_scales.bitcast(I32)
         for q in range(4):
             nc.sync.dma_start(
@@ -78,13 +82,18 @@ def tile_differencetargetpropweightstep_d1p_kernel(
         nc.scalar.dma_start(out=c_bf[:], in_=c.rearrange("(g p t) -> p g t", g=2, p=P, t=4))
         x_sc = keep("x_sc", [P, 2, 32], F32)
         nc.scalar.dma_start(out=x_sc[:], in_=x_scale.rearrange("(g p t) j -> p g (t j)", g=2, p=P, t=4))
+        v_w = [keep("v_w%d" % g, [P, SIZE], U32) for g in range(2)]
+
+        def load_v(half):
+            cols = slice(512 * half, 512 * (half + 1))
+            for g in range(2):
+                words = v_words[g].rearrange("p n t -> p (n t)").bitcast(I32)
+                nc.sync.dma_start(out=v_w[g][:, cols].bitcast(I32), in_=words[:, cols])
+
         load_bf16("h", h, 0, (2, 2))
-        v_w = []
-        for g in range(2):
-            tl = keep("v_w%d" % g, [P, SIZE], U32)
-            nc.sync.dma_start(out=tl[:].bitcast(I32), in_=v_words[g].rearrange("p n t -> p (n t)").bitcast(I32))
-            v_w.append(tl)
+        load_v(0)
         load_x(0)
+        load_v(1)
         load_cols("a", a, 0, 0)
         load_bf16("t", t, 1, (4,))
         load_cols("a", a, 0, 1)
@@ -137,23 +146,29 @@ def tile_differencetargetpropweightstep_d1p_kernel(
                 in_=grouped[key, g][:, gk, :, :].rearrange("p r f -> p (r f)"),
             )
 
+        def warm_pe(n, width, tag="m"):
+            for i in range(n):
+                ps = psum.tile([P, 512], F32, name="warm_ps", tag=tag, bufs=4)
+                nc.tensor.matmul(ps[:, 0:width], lhsT=zeros[:, 0:P], rhs=zeros[:, 0:width], start=True, stop=True)
+
         x_codes = {}
         x_scales = {}
         x_plane = {}
         x_inter = {}
 
         def x_widen(g, hf, s):
+            on_scalar = s in SCALAR_WIDENS
             if s == 0:
                 x_plane[g, hf] = work.tile([P, 4, 512], BF16, name="x_plane", tag="x_plane")
             for j in range(4):
                 cols = slice(512 * hf + P * j, 512 * hf + P * (j + 1))
-                nc.vector.tensor_scalar(
-                    out=x_plane[g, hf][:, s, P * j : P * (j + 1)],
-                    in0=x_b[g][:, s, cols].bitcast(FP8),
-                    scalar1=x_sc[:, g, 8 * s + 4 * hf + j : 8 * s + 4 * hf + j + 1],
-                    scalar2=None,
-                    op0=ALU.mult,
-                )
+                dst = x_plane[g, hf][:, s, P * j : P * (j + 1)]
+                src = x_b[g][:, s, cols].bitcast(FP8)
+                scale = x_sc[:, g, 8 * s + 4 * hf + j : 8 * s + 4 * hf + j + 1]
+                if on_scalar:
+                    nc.scalar.activation(out=dst, in_=src, func=ACT.Copy, scale=scale)
+                else:
+                    nc.vector.tensor_scalar(out=dst, in0=src, scalar1=scale, scalar2=None, op0=ALU.mult)
 
         def x_interleave(g, hf):
             x_inter[g, hf] = work.tile([P, 512, 4], BF16, name="x_inter", tag="x_inter", align_bytes=64)
@@ -208,7 +223,7 @@ def tile_differencetargetpropweightstep_d1p_kernel(
                     start=(gk == 0),
                     stop=(gk == 1),
                 )
-            tl = work.tile([P, 512], F32, name="tanh_" + key, tag="tanh_" + key, bufs=5)
+            tl = work.tile([P, 512], F32, name="tanh_" + key, tag="tanh_" + key, bufs=9 if key == "t" else 5)
             tanh_tiles[r, u, key] = tl
             nc.scalar.activation(
                 out=tl[:],
@@ -217,6 +232,12 @@ def tile_differencetargetpropweightstep_d1p_kernel(
                 bias=bias[:, db : db + 1] if key == "t" else nbias[:, db : db + 1],
                 scale=1.0 if key == "t" else -1.0,
             )
+
+        def subtract(r):
+            for u in range(2):
+                tl = work.tile([P, 512], F32, name="diff", tag="diff", bufs=4)
+                nc.vector.tensor_tensor(out=tl[:], in0=tanh_tiles[r, u, "t"][:], in1=tanh_tiles[r, u, "h"][:], op=ALU.add)
+                tanh_tiles[r, u, "e"] = tl
 
         def sigmoid(r):
             g, dp = divmod(r, 4)
@@ -227,6 +248,16 @@ def tile_differencetargetpropweightstep_d1p_kernel(
             g = r // 4
             weight[r] = work.tile([P, 4, 256], F32, name="weight", tag="weight", bufs=2)
             for s in range(4):
+                if r in GP_ROUNDS:
+                    nc.gpsimd.tensor_scalar(
+                        out=weight[r][:, s, :],
+                        in0=sig[r][:, s, :],
+                        scalar1=c32[:, g, s : s + 1],
+                        scalar2=0.0,
+                        op0=ALU.mult,
+                        op1=ALU.add,
+                    )
+                    continue
                 nc.vector.tensor_scalar(
                     out=weight[r][:, s, :], in0=sig[r][:, s, :], scalar1=c32[:, g, s : s + 1], scalar2=None, op0=ALU.mult
                 )
@@ -236,14 +267,15 @@ def tile_differencetargetpropweightstep_d1p_kernel(
                 ps = psum.tile([P, 4, P], F32, name="e_ps", tag="m", bufs=4)
                 e_ps[r, u] = ps
                 for s in range(4):
-                    for key in ("t", "h"):
+                    parts = ["e"] if (r, u, "e") in tanh_tiles else ["t", "h"]
+                    for key in parts:
                         nc.tensor.matmul(
                             ps[:, s, :],
                             lhsT=tanh_tiles[r, u, key][:, P * s : P * (s + 1)],
                             rhs=ident[:],
                             is_transpose=True,
-                            start=(key == "t"),
-                            stop=(key == "h"),
+                            start=(key == parts[0]),
+                            stop=(key == parts[-1]),
                         )
 
         def error(r):
@@ -290,12 +322,15 @@ def tile_differencetargetpropweightstep_d1p_kernel(
                     nc.vector.tensor_scalar(out=res[:], in0=ps[:], scalar1=1.0 / 32.0, scalar2=None, op0=ALU.mult)
                 nc.sync.dma_start(out=out_view[:, 2 * ep : 2 * ep + 2, 256 * j : 256 * (j + 1)], in_=res[:])
 
+        warm_pe(3, 512)
         for s in range(4):
             turn_slot("t", 0, s, "z", "vs"[s % 2])
+            pass
             if s == 1:
                 small_vectors()
         for s in range(4):
             turn_slot("h", 0, s, "m", "sv"[s % 2])
+            pass
             if s == 1:
                 quantise_th("t", 0, 0)
             if s == 3:
@@ -304,28 +339,36 @@ def tile_differencetargetpropweightstep_d1p_kernel(
         quantise_th("h", 0, 1)
         do_x(8)
         late = [(key, s) for key in ("t", "h") for s in range(4)]
-        late_by_step = {1: late[0:3], 2: late[3:6], 3: late[6:8]}
+        mid = {1:(0,1),2:(3,4),3:(6,7)}
+        end = {1:(1,3),2:(4,6),3:(7,8)}
+        xa = {1:3,2:2,3:2,4:2,5:1}
+        xb = {1:2,2:1,3:1,4:2,5:3}
         for step in range(10):
             if step < 8:
                 for key in ("t", "h"):
                     for u in range(2):
                         forward(step, u, key)
+                    if key == "t":
+                        for i, (k2, s) in enumerate(late[slice(*mid.get(step, (0, 0)))]):
+                            turn_slot(k2, 1, s, "m", "s")
                 sigmoid(step)
             if 1 <= step <= 8:
                 if step == 3:
                     quantise_th("t", 1, 0)
                     quantise_th("t", 1, 1)
                 row_weight(step - 1)
-                do_x(((0, 2,2,2,2,2) + (0,) * 9)[step])
+                do_x(xa.get(step, 0))
                 back(step - 1)
                 error(step - 1)
-            for i, (key, s) in enumerate(late_by_step.get(step, [])):
-                turn_slot(key, 1, s, "m", "sss"[i])
+            for i, (k2, s) in enumerate(late[slice(*end.get(step, (0, 0)))]):
+                turn_slot(k2, 1, s, "m", "s")
             if step == 3:
                 quantise_th("h", 1, 0)
                 quantise_th("h", 1, 1)
             if 1 <= step <= 8:
                 quantise_q(step - 1)
-                do_x(((0, 2,2,2,2,2) + (0,) * 9)[step])
+                if step in ():
+                    subtract(step)
+                do_x(xb.get(step, 0))
             if step >= 6:
                 final(step - 6)

@@ -96,9 +96,9 @@ def tile_differencetargetpropweightstep_d1p_kernel(
         load_v(1)
         load_cols("a", a, 0, 0)
         load_bf16("t", t, 1, (4,))
+        load_x(1)
         load_cols("a", a, 0, 1)
         load_bf16("h", h, 1, (4,))
-        load_x(1)
         load_cols("a", a, 1, 0)
         load_cols("a", a, 1, 1)
 
@@ -262,8 +262,8 @@ def tile_differencetargetpropweightstep_d1p_kernel(
                     out=weight[r][:, s, :], in0=sig[r][:, s, :], scalar1=c32[:, g, s : s + 1], scalar2=None, op0=ALU.mult
                 )
 
-        def back(r):
-            for u in range(2):
+        def back(r, units=(0, 1)):
+            for u in units:
                 ps = psum.tile([P, 4, P], F32, name="e_ps", tag="m", bufs=4)
                 e_ps[r, u] = ps
                 for s in range(4):
@@ -278,9 +278,10 @@ def tile_differencetargetpropweightstep_d1p_kernel(
                             stop=(key == parts[-1]),
                         )
 
-        def error(r):
-            q_in[r] = work.tile([P, 256, 4], BF16, name="q_in", tag="q_in", align_bytes=64)
-            for u in range(2):
+        def error(r, units=(0, 1)):
+            if 0 in units:
+                q_in[r] = work.tile([P, 256, 4], BF16, name="q_in", tag="q_in", align_bytes=64)
+            for u in units:
                 nc.vector.tensor_tensor(
                     out=q_in[r][:, P * u : P * (u + 1), :],
                     in0=e_ps[r, u][:].rearrange("p s d -> p d s"),
@@ -322,52 +323,68 @@ def tile_differencetargetpropweightstep_d1p_kernel(
                     nc.vector.tensor_scalar(out=res[:], in0=ps[:], scalar1=1.0 / 32.0, scalar2=None, op0=ALU.mult)
                 nc.sync.dma_start(out=out_view[:, 2 * ep : 2 * ep + 2, 256 * j : 256 * (j + 1)], in_=res[:])
 
-        warm_pe(3, 512)
+        warm_pe(5, 512)
         for s in range(4):
-            turn_slot("t", 0, s, "z", "vs"[s % 2])
-            pass
+            turn_slot("t", 0, s, "z", "ssss"[s])
+            if s in (0, 1, 2, 3):
+                warm_pe(1, 512)
             if s == 1:
                 small_vectors()
         for s in range(4):
-            turn_slot("h", 0, s, "m", "sv"[s % 2])
-            pass
+            if s == 0 and 0 > 0:
+                if s == 0:
+                    quantise_th("t", 0, 0)
+                    quantise_th("t", 0, 1)
+                for k in range(0):
+                    forward(k // 2, k % 2, "t")
+            turn_slot("h", 0, s, "m", "vsvs"[s])
+            if s in (0, 2):
+                warm_pe(1, 512, "z")
             if s == 1:
                 quantise_th("t", 0, 0)
-            if s == 3:
+            if s == 2:
                 quantise_th("t", 0, 1)
         quantise_th("h", 0, 0)
         quantise_th("h", 0, 1)
         do_x(8)
         late = [(key, s) for key in ("t", "h") for s in range(4)]
-        mid = {1:(0,1),2:(3,4),3:(6,7)}
-        end = {1:(1,3),2:(4,6),3:(7,8)}
-        xa = {1:3,2:2,3:2,4:2,5:1}
-        xb = {1:2,2:1,3:1,4:2,5:3}
+        mid = {2:(2,4),3:(6,8)}
+        end = {1:(0,2),2:(4,6)}
+        xa = {1:3,2:3,3:3,4:0,5:1}
+        xb = {1:2,2:4,3:2,4:4,5:4}
         for step in range(10):
+            if step == 3:
+                quantise_th("t", 1, 0)
+                quantise_th("t", 1, 1)
+            if 1 <= step <= 8:
+                row_weight(step - 1)
             if step < 8:
                 for key in ("t", "h"):
                     for u in range(2):
                         forward(step, u, key)
                     if key == "t":
+                        if step in (99,):
+                            do_x(xa.get(step, 0))
+                            back(step - 1)
+                            error(step - 1)
                         for i, (k2, s) in enumerate(late[slice(*mid.get(step, (0, 0)))]):
-                            turn_slot(k2, 1, s, "m", "s")
+                            turn_slot(k2, 1, s, "m", "ssss"[s])
+                            if k2 == "h" and s == 3:
+                                quantise_th("h", 1, 0)
+                                quantise_th("h", 1, 1)
                 sigmoid(step)
-            if 1 <= step <= 8:
-                if step == 3:
-                    quantise_th("t", 1, 0)
-                    quantise_th("t", 1, 1)
-                row_weight(step - 1)
+            if 1 <= step <= 8 and step not in (99,):
                 do_x(xa.get(step, 0))
                 back(step - 1)
                 error(step - 1)
             for i, (k2, s) in enumerate(late[slice(*end.get(step, (0, 0)))]):
-                turn_slot(k2, 1, s, "m", "s")
-            if step == 3:
-                quantise_th("h", 1, 0)
-                quantise_th("h", 1, 1)
+                turn_slot(k2, 1, s, "m", "ssss"[s])
+                if k2 == "h" and s == 3:
+                    quantise_th("h", 1, 0)
+                    quantise_th("h", 1, 1)
             if 1 <= step <= 8:
                 quantise_q(step - 1)
-                if step in ():
+                if step in (5,6,7):
                     subtract(step)
                 do_x(xb.get(step, 0))
             if step >= 6:

@@ -15,7 +15,7 @@ ALU = mybir.AluOpType
 
 P = 128
 SIZE = 1024
-SCALAR_WIDENS = ()
+SCALAR_WIDENS = (3,)
 GP_ROUNDS = (0, 1, 2, 3, 4, 5, 6, 7)
 FLOPS = 3 * 2 * SIZE * SIZE * SIZE
 
@@ -70,18 +70,25 @@ def tile_differencetargetpropweightstep_d1p_kernel(
             x_b.append(tl)
 
         load_bf16("t", t, 0, (1, 1, 2))
-        nc.scalar.activation(out=warm[:], in_=zeros[:, 0:2], func=ACT.Sigmoid)
         vs32 = v_scales.bitcast(I32)
         for q in range(4):
-            nc.sync.dma_start(
+            nc.scalar.dma_start(
                 out=v_sc[32 * q : 32 * q + 8, :].bitcast(I32),
                 in_=vs32[:, 4 * q : 4 * q + 4, :],
             )
-        nc.scalar.dma_start(out=b_rows[0:8, :], in_=b.rearrange("(j p) -> j p", p=P))
         c_bf = keep("c_bf", [P, 2, 4], BF16)
-        nc.scalar.dma_start(out=c_bf[:], in_=c.rearrange("(g p t) -> p g t", g=2, p=P, t=4))
         x_sc = keep("x_sc", [P, 2, 32], F32)
-        nc.scalar.dma_start(out=x_sc[:], in_=x_scale.rearrange("(g p t) j -> p g (t j)", g=2, p=P, t=4))
+
+        def load_b():
+            nc.sync.dma_start(out=b_rows[0:8, :], in_=b.rearrange("(j p) -> j p", p=P))
+
+        def load_c():
+            nc.sync.dma_start(out=c_bf[:], in_=c.rearrange("(g p t) -> p g t", g=2, p=P, t=4))
+
+        def load_xs():
+            nc.sync.dma_start(out=x_sc[:], in_=x_scale.rearrange("(g p t) j -> p g (t j)", g=2, p=P, t=4))
+
+        nc.scalar.activation(out=warm[:], in_=zeros[:, 0:2], func=ACT.Sigmoid)
         v_w = [keep("v_w%d" % g, [P, SIZE], U32) for g in range(2)]
 
         def load_v(half):
@@ -91,24 +98,25 @@ def tile_differencetargetpropweightstep_d1p_kernel(
                 nc.sync.dma_start(out=v_w[g][:, cols].bitcast(I32), in_=words[:, cols])
 
         load_bf16("h", h, 0, (2, 2))
+        load_b()
         load_v(0)
         load_x(0)
-        load_v(1)
+        load_xs()
         load_cols("a", a, 0, 0)
+        load_v(1)
+        load_c()
         load_bf16("t", t, 1, (4,))
         load_x(1)
-        load_cols("a", a, 0, 1)
         load_bf16("h", h, 1, (4,))
+        load_cols("a", a, 0, 1)
         load_cols("a", a, 1, 0)
         load_cols("a", a, 1, 1)
 
-        c32 = keep("c32", [P, 2, 4], F32)
         b_f32 = keep("b_f32", [P, P], F32)
         bias = keep("bias", [P, 8], F32)
         nbias = keep("nbias", [P, 8], F32)
 
         def small_vectors():
-            nc.vector.tensor_copy(out=c32[:], in_=c_bf[:])
             nc.vector.tensor_copy(out=b_f32[:], in_=b_rows[:])
             b_ps = psum.tile([P, 512], F32, name="b_ps", tag="m", bufs=4)
             nc.tensor.transpose(b_ps[:, 0:P], b_f32[:], ident[:])
@@ -223,7 +231,7 @@ def tile_differencetargetpropweightstep_d1p_kernel(
                     start=(gk == 0),
                     stop=(gk == 1),
                 )
-            tl = work.tile([P, 512], F32, name="tanh_" + key, tag="tanh_" + key, bufs=9 if key == "t" else 5)
+            tl = work.tile([P, 512], F32, name="tanh_" + key, tag="tanh_" + key, bufs=5)
             tanh_tiles[r, u, key] = tl
             nc.scalar.activation(
                 out=tl[:],
@@ -252,14 +260,14 @@ def tile_differencetargetpropweightstep_d1p_kernel(
                     nc.gpsimd.tensor_scalar(
                         out=weight[r][:, s, :],
                         in0=sig[r][:, s, :],
-                        scalar1=c32[:, g, s : s + 1],
+                        scalar1=c_bf[:, g, s : s + 1],
                         scalar2=0.0,
                         op0=ALU.mult,
                         op1=ALU.add,
                     )
                     continue
                 nc.vector.tensor_scalar(
-                    out=weight[r][:, s, :], in0=sig[r][:, s, :], scalar1=c32[:, g, s : s + 1], scalar2=None, op0=ALU.mult
+                    out=weight[r][:, s, :], in0=sig[r][:, s, :], scalar1=c_bf[:, g, s : s + 1], scalar2=None, op0=ALU.mult
                 )
 
         def back(r, units=(0, 1)):
@@ -301,11 +309,11 @@ def tile_differencetargetpropweightstep_d1p_kernel(
         out_view = out.rearrange("(e p) d -> p e d", p=P)
 
         def final(j):
-            for ep in range(4):
-                ps = psum.tile([P, 2, 256], F32, name="o_ps", tag="m", bufs=4)
-                for i in range(2):
-                    eb = 2 * ep + i
-                    hf, el = divmod(eb, 4)
+            width = 1 if j == 3 else 2
+            for n in range(8 // width):
+                ps = psum.tile([P, width, 256], F32, name="o_ps", tag="m", bufs=4)
+                for i in range(width):
+                    hf, el = divmod(width * n + i, 4)
                     for g in range(2):
                         nc.tensor.matmul_mx(
                             out=ps[:, i, :],
@@ -316,20 +324,18 @@ def tile_differencetargetpropweightstep_d1p_kernel(
                             start=(g == 0),
                             stop=(g == 1),
                         )
-                res = work.tile([P, 2, 256], F32, name="res", tag="res", bufs=8)
-                if ep % 2 == 0:
+                res = work.tile([P, width, 256], F32, name="res", tag="res%d" % width, bufs=8 if width == 1 else 12)
+                if n % 2 == 0:
                     nc.scalar.activation(out=res[:], in_=ps[:], func=ACT.Copy, scale=1.0 / 32.0)
                 else:
                     nc.vector.tensor_scalar(out=res[:], in0=ps[:], scalar1=1.0 / 32.0, scalar2=None, op0=ALU.mult)
-                nc.sync.dma_start(out=out_view[:, 2 * ep : 2 * ep + 2, 256 * j : 256 * (j + 1)], in_=res[:])
+                nc.sync.dma_start(out=out_view[:, width * n : width * (n + 1), 256 * j : 256 * (j + 1)], in_=res[:])
 
         warm_pe(5, 512)
         for s in range(4):
             turn_slot("t", 0, s, "z", "ssss"[s])
             if s in (0, 1, 2, 3):
                 warm_pe(1, 512)
-            if s == 1:
-                small_vectors()
         for s in range(4):
             if s == 0 and 0 > 0:
                 if s == 0:
@@ -337,12 +343,14 @@ def tile_differencetargetpropweightstep_d1p_kernel(
                     quantise_th("t", 0, 1)
                 for k in range(0):
                     forward(k // 2, k % 2, "t")
-            turn_slot("h", 0, s, "m", "vsvs"[s])
-            if s in (0, 2):
+            turn_slot("h", 0, s, "m", "ssss"[s])
+            if s == 3:
+                small_vectors()
+            if s in (2, 3):
                 warm_pe(1, 512, "z")
             if s == 1:
                 quantise_th("t", 0, 0)
-            if s == 2:
+            if s == 3:
                 quantise_th("t", 0, 1)
         quantise_th("h", 0, 0)
         quantise_th("h", 0, 1)
@@ -350,8 +358,8 @@ def tile_differencetargetpropweightstep_d1p_kernel(
         late = [(key, s) for key in ("t", "h") for s in range(4)]
         mid = {2:(2,4),3:(6,8)}
         end = {1:(0,2),2:(4,6)}
-        xa = {1:3,2:3,3:3,4:0,5:1}
-        xb = {1:2,2:4,3:2,4:4,5:4}
+        xa = {1:3,2:1,3:0,4:1,5:1}
+        xb = {1:3,2:4,3:3,4:2,5:0}
         for step in range(10):
             if step == 3:
                 quantise_th("t", 1, 0)
@@ -368,7 +376,7 @@ def tile_differencetargetpropweightstep_d1p_kernel(
                             back(step - 1)
                             error(step - 1)
                         for i, (k2, s) in enumerate(late[slice(*mid.get(step, (0, 0)))]):
-                            turn_slot(k2, 1, s, "m", "ssss"[s])
+                            turn_slot(k2, 1, s, "m", "svss"[s])
                             if k2 == "h" and s == 3:
                                 quantise_th("h", 1, 0)
                                 quantise_th("h", 1, 1)
@@ -378,7 +386,7 @@ def tile_differencetargetpropweightstep_d1p_kernel(
                 back(step - 1)
                 error(step - 1)
             for i, (k2, s) in enumerate(late[slice(*end.get(step, (0, 0)))]):
-                turn_slot(k2, 1, s, "m", "ssss"[s])
+                turn_slot(k2, 1, s, "m", "svss"[s])
                 if k2 == "h" and s == 3:
                     quantise_th("h", 1, 0)
                     quantise_th("h", 1, 1)

@@ -99,14 +99,14 @@ def tile_differencetargetpropweightstep_d1p_kernel(
 
         load_bf16("h", h, 0, (2, 2))
         load_b()
-        load_v(0)
         load_x(0)
         load_xs()
+        load_v(0)
+        load_x(1)
         load_cols("a", a, 0, 0)
-        load_v(1)
         load_c()
         load_bf16("t", t, 1, (4,))
-        load_x(1)
+        load_v(1)
         load_bf16("h", h, 1, (4,))
         load_cols("a", a, 0, 1)
         load_cols("a", a, 1, 0)
@@ -192,7 +192,7 @@ def tile_differencetargetpropweightstep_d1p_kernel(
             )
 
         x_work = []
-        chunks = [(g, hf) for g in range(2) for hf in range(2)]
+        chunks = [(g, hf) for hf in range(2) for g in range(2)]
         for i in range(5):
             for s in range(4):
                 if i < 4:
@@ -308,12 +308,12 @@ def tile_differencetargetpropweightstep_d1p_kernel(
 
         out_view = out.rearrange("(e p) d -> p e d", p=P)
 
-        def final(j):
+        def final(j, hf):
             width = 1 if j == 3 else 2
-            for n in range(8 // width):
+            for n in range(4 // width):
                 ps = psum.tile([P, width, 256], F32, name="o_ps", tag="m", bufs=4)
                 for i in range(width):
-                    hf, el = divmod(width * n + i, 4)
+                    el = width * n + i
                     for g in range(2):
                         nc.tensor.matmul_mx(
                             out=ps[:, i, :],
@@ -329,12 +329,13 @@ def tile_differencetargetpropweightstep_d1p_kernel(
                     nc.scalar.activation(out=res[:], in_=ps[:], func=ACT.Copy, scale=1.0 / 32.0)
                 else:
                     nc.vector.tensor_scalar(out=res[:], in0=ps[:], scalar1=1.0 / 32.0, scalar2=None, op0=ALU.mult)
-                nc.sync.dma_start(out=out_view[:, width * n : width * (n + 1), 256 * j : 256 * (j + 1)], in_=res[:])
+                e0 = 4 * hf + width * n
+                nc.sync.dma_start(out=out_view[:, e0 : e0 + width, 256 * j : 256 * (j + 1)], in_=res[:])
 
-        warm_pe(5, 512)
+        warm_pe(6, 512)
         for s in range(4):
             turn_slot("t", 0, s, "z", "ssss"[s])
-            if s in (0, 1, 2, 3):
+            if s in (1, 3):
                 warm_pe(1, 512)
         for s in range(4):
             if s == 0 and 0 > 0:
@@ -346,7 +347,7 @@ def tile_differencetargetpropweightstep_d1p_kernel(
             turn_slot("h", 0, s, "m", "ssss"[s])
             if s == 3:
                 small_vectors()
-            if s in (2, 3):
+            if s in (0, 2):
                 warm_pe(1, 512, "z")
             if s == 1:
                 quantise_th("t", 0, 0)
@@ -354,12 +355,12 @@ def tile_differencetargetpropweightstep_d1p_kernel(
                 quantise_th("t", 0, 1)
         quantise_th("h", 0, 0)
         quantise_th("h", 0, 1)
-        do_x(8)
+        do_x(6)
         late = [(key, s) for key in ("t", "h") for s in range(4)]
         mid = {2:(2,4),3:(6,8)}
         end = {1:(0,2),2:(4,6)}
-        xa = {1:3,2:1,3:0,4:1,5:1}
-        xb = {1:3,2:4,3:3,4:2,5:0}
+        xa = {1:1,2:2,3:0,4:0,5:0,6:2}
+        xb = {1:3,2:1,3:2,4:3,5:1,6:3}
         for step in range(10):
             if step == 3:
                 quantise_th("t", 1, 0)
@@ -376,7 +377,7 @@ def tile_differencetargetpropweightstep_d1p_kernel(
                             back(step - 1)
                             error(step - 1)
                         for i, (k2, s) in enumerate(late[slice(*mid.get(step, (0, 0)))]):
-                            turn_slot(k2, 1, s, "m", "svss"[s])
+                            turn_slot(k2, 1, s, "m", "vvss"[s])
                             if k2 == "h" and s == 3:
                                 quantise_th("h", 1, 0)
                                 quantise_th("h", 1, 1)
@@ -386,14 +387,14 @@ def tile_differencetargetpropweightstep_d1p_kernel(
                 back(step - 1)
                 error(step - 1)
             for i, (k2, s) in enumerate(late[slice(*end.get(step, (0, 0)))]):
-                turn_slot(k2, 1, s, "m", "svss"[s])
+                turn_slot(k2, 1, s, "m", "vvss"[s])
                 if k2 == "h" and s == 3:
                     quantise_th("h", 1, 0)
                     quantise_th("h", 1, 1)
             if 1 <= step <= 8:
                 quantise_q(step - 1)
-                if step in (5,6,7):
+                if step in ():
                     subtract(step)
                 do_x(xb.get(step, 0))
-            if step >= 6:
-                final(step - 6)
+            for j, hf in {6: [(0, 0)], 7: [(0, 1), (1, 0)], 8: [(1, 1), (2, 0), (2, 1)], 9: [(3, 0), (3, 1)]}.get(step, ()):
+                final(j, hf)

from contextlib import ExitStack

import concourse.mybir as mybir
from concourse.masks import make_identity

F32 = mybir.dt.float32
BF16 = mybir.dt.bfloat16
I32 = mybir.dt.int32
U32 = mybir.dt.uint32
U8 = mybir.dt.uint8
FP8 = mybir.dt.float8_e4m3fn
FP8X4 = mybir.dt.float8_e4m3fn_x4
ACT = mybir.ActivationFunctionType
ALU = mybir.AluOpType

P = 128
SIZE = 1024
SCALAR_WIDENS = (3,)
GP_ROUNDS = (0, 1, 2, 3, 4, 5, 6, 7)
FLOPS = 3 * 2 * SIZE * SIZE * SIZE


def tile_differencetargetpropweightstep_d1p_kernel(
    tc, t, h, v_words, v_scales, b, a, x_bytes, x_scale, c, out
):
    nc = tc.nc
    with ExitStack() as ctx:
        const = ctx.enter_context(tc.tile_pool(name="const", bufs=1))
        work = ctx.enter_context(tc.tile_pool(name="work", bufs=2))
        psum = ctx.enter_context(tc.psum_pool(name="psum", bufs=2))
        ctx.enter_context(tc.manual_schedule())

        def keep(name, shape, dtype):
            return const.tile(shape, dtype, name=name, align_bytes=64)

        ident = keep("ident", [P, P], F32)
        make_identity(nc, ident[:])
        v_sc = keep("v_sc", [P, SIZE], U8)
        nc.vector.memset(v_sc[:].bitcast(I32), 0)
        b_rows = keep("b_rows", [P, P], BF16)
        nc.vector.memset(b_rows[:], 0.0)
        warm = keep("warm", [P, 2], F32)
        zeros = keep("zeros", [P, 512], BF16)
        nc.vector.memset(zeros[:], 0.0)

        def rows4(ap):
            return ap.rearrange("(g p t) k -> g p t k", g=2, p=P, t=4)

        raw = {}

        def load_bf16(key, ap, g, parts):
            tl = keep("raw_%s%d" % (key, g), [P, 4, SIZE], BF16)
            raw[key, g] = tl
            s = 0
            for n in parts:
                nc.sync.dma_start(out=tl[:, s : s + n, :], in_=rows4(ap)[g][:, s : s + n, :])
                s += n

        def load_cols(key, ap, g, half):
            if half == 0:
                raw[key, g] = keep("raw_%s%d" % (key, g), [P, 4, SIZE], BF16)
            cols = slice(512 * half, 512 * (half + 1))
            nc.sync.dma_start(out=raw[key, g][:, :, cols], in_=rows4(ap)[g][:, :, cols])

        x_b = []

        def load_x(g):
            tl = keep("x_b%d" % g, [P, 4, SIZE], U8)
            nc.sync.dma_start(out=tl[:], in_=rows4(x_bytes)[g])
            x_b.append(tl)

        load_bf16("t", t, 0, (1, 1, 2))
        vs32 = v_scales.bitcast(I32)
        for q in range(4):
            nc.scalar.dma_start(
                out=v_sc[32 * q : 32 * q + 8, :].bitcast(I32),
                in_=vs32[:, 4 * q : 4 * q + 4, :],
            )
        c_bf = keep("c_bf", [P, 2, 4], BF16)
        x_sc = keep("x_sc", [P, 2, 32], F32)

        def load_b():
            nc.sync.dma_start(out=b_rows[0:8, :], in_=b.rearrange("(j p) -> j p", p=P))

        def load_c():
            nc.sync.dma_start(out=c_bf[:], in_=c.rearrange("(g p t) -> p g t", g=2, p=P, t=4))

        def load_xs():
            nc.sync.dma_start(out=x_sc[:], in_=x_scale.rearrange("(g p t) j -> p g (t j)", g=2, p=P, t=4))

        nc.scalar.activation(out=warm[:], in_=zeros[:, 0:2], func=ACT.Sigmoid)
        v_w = [keep("v_w%d" % g, [P, SIZE], U32) for g in range(2)]

        def load_v(half):
            cols = slice(512 * half, 512 * (half + 1))
            for g in range(2):
                words = v_words[g].rearrange("p n t -> p (n t)").bitcast(I32)
                nc.sync.dma_start(out=v_w[g][:, cols].bitcast(I32), in_=words[:, cols])

        load_bf16("h", h, 0, (2, 2))
        load_b()
        load_x(0)
        load_xs()
        load_v(0)
        load_x(1)
        load_cols("a", a, 0, 0)
        load_c()
        load_bf16("t", t, 1, (4,))
        load_v(1)
        load_bf16("h", h, 1, (4,))
        load_cols("a", a, 0, 1)
        load_cols("a", a, 1, 0)
        load_cols("a", a, 1, 1)

        b_f32 = keep("b_f32", [P, P], F32)
        bias = keep("bias", [P, 8], F32)
        nbias = keep("nbias", [P, 8], F32)

        def small_vectors():
            nc.vector.tensor_copy(out=b_f32[:], in_=b_rows[:])
            b_ps = psum.tile([P, 512], F32, name="b_ps", tag="m", bufs=4)
            nc.tensor.transpose(b_ps[:, 0:P], b_f32[:], ident[:])
            nc.vector.tensor_copy(out=bias[:], in_=b_ps[:, 0:8])
            nc.vector.tensor_scalar(out=nbias[:], in0=b_ps[:, 0:8], scalar1=-1.0, scalar2=None, op0=ALU.mult)


        grouped = {}
        codes = {}
        scales = {}

        def turn_slot(key, g, s, tag, engine):
            if s == 0:
                grouped[key, g] = work.tile([P, 2, 512, 4], BF16, name="grouped", tag="grouped", bufs=3, align_bytes=64)
            words = raw[key, g][:, s, :].bitcast(F32)
            ps = psum.tile([P, 2, 2, P], F32, name="turn_ps", tag=tag, bufs=4)
            for gk in range(2):
                for u in range(2):
                    nc.tensor.transpose(ps[:, gk, u, :], words[:, 256 * gk + u : 256 * (gk + 1) : 2], ident[:])
            dst = grouped[key, g][:, :, P * s : P * (s + 1), :].rearrange("p k r f -> p k (r f)").bitcast(F32)
            dst = dst.rearrange("p k (r u) -> p k r u", u=2)
            src = ps[:].rearrange("p k u r -> p k r u")
            if engine == "v":
                nc.vector.tensor_copy(out=dst, in_=src)
            else:
                nc.scalar.copy(out=dst, in_=src)

        def quantise_th(key, g, gk):
            if gk == 0:
                codes[key, g] = keep("codes_%s%d" % (key, g), [P, 2, 512], U32)
                scales[key, g] = keep("scales_%s%d" % (key, g), [P, 2, 512], U8)
            nc.vector.quantize_mx(
                out=codes[key, g][:, gk, :].bitcast(FP8X4),
                scales=scales[key, g][:, gk, :],
                in_=grouped[key, g][:, gk, :, :].rearrange("p r f -> p (r f)"),
            )

        def warm_pe(n, width, tag="m"):
            for i in range(n):
                ps = psum.tile([P, 512], F32, name="warm_ps", tag=tag, bufs=4)
                nc.tensor.matmul(ps[:, 0:width], lhsT=zeros[:, 0:P], rhs=zeros[:, 0:width], start=True, stop=True)

        x_codes = {}
        x_scales = {}
        x_plane = {}
        x_inter = {}

        def x_widen(g, hf, s):
            on_scalar = s in SCALAR_WIDENS
            if s == 0:
                x_plane[g, hf] = work.tile([P, 4, 512], BF16, name="x_plane", tag="x_plane")
            for j in range(4):
                cols = slice(512 * hf + P * j, 512 * hf + P * (j + 1))
                dst = x_plane[g, hf][:, s, P * j : P * (j + 1)]
                src = x_b[g][:, s, cols].bitcast(FP8)
                scale = x_sc[:, g, 8 * s + 4 * hf + j : 8 * s + 4 * hf + j + 1]
                if on_scalar:
                    nc.scalar.activation(out=dst, in_=src, func=ACT.Copy, scale=scale)
                else:
                    nc.vector.tensor_scalar(out=dst, in0=src, scalar1=scale, scalar2=None, op0=ALU.mult)

        def x_interleave(g, hf):
            x_inter[g, hf] = work.tile([P, 512, 4], BF16, name="x_inter", tag="x_inter", align_bytes=64)
            nc.vector.tensor_copy(out=x_inter[g, hf][:], in_=x_plane[g, hf][:].rearrange("p s e -> p e s"))

        def x_quantise(g, hf):
            x_codes[g, hf] = keep("x_codes%d%d" % (g, hf), [P, 512], U32)
            x_scales[g, hf] = keep("x_scales%d%d" % (g, hf), [P, 512], U8)
            nc.vector.quantize_mx(
                out=x_codes[g, hf][:].bitcast(FP8X4),
                scales=x_scales[g, hf][:],
                in_=x_inter[g, hf][:].rearrange("p e s -> p (e s)"),
            )

        x_work = []
        chunks = [(g, hf) for hf in range(2) for g in range(2)]
        for i in range(5):
            for s in range(4):
                if i < 4:
                    x_work.append((x_widen, (*chunks[i], s)))
                if i > 0 and s == 0:
                    x_work.append((x_interleave, chunks[i - 1]))
                if i > 0 and s == 1:
                    x_work.append((x_quantise, chunks[i - 1]))

        def do_x(n):
            for fn, args in x_work[:n]:
                fn(*args)
            del_list = x_work[n:]
            x_work.clear()
            x_work.extend(del_list)

        tanh_tiles = {}
        sig = {}
        weight = {}
        e_ps = {}
        q_in = {}
        q_codes = {}
        q_scales = {}

        def forward(r, u, key):
            g, dp = divmod(r, 4)
            db = 2 * dp + u
            z = psum.tile([P, 512], F32, name="z", tag="z", bufs=4)
            for gk in range(2):
                nc.tensor.matmul_mx(
                    out=z[:],
                    lhsT=v_w[gk][:, P * db : P * (db + 1)].bitcast(FP8X4),
                    lhsT_scale=v_sc[4 * gk : P, P * db : P * (db + 1)],
                    rhs=codes[key, g][:, gk, :].bitcast(FP8X4),
                    rhs_scale=scales[key, g][:, gk, :],
                    start=(gk == 0),
                    stop=(gk == 1),
                )
            tl = work.tile([P, 512], F32, name="tanh_" + key, tag="tanh_" + key, bufs=5)
            tanh_tiles[r, u, key] = tl
            nc.scalar.activation(
                out=tl[:],
                in_=z[:],
                func=ACT.Tanh,
                bias=bias[:, db : db + 1] if key == "t" else nbias[:, db : db + 1],
                scale=1.0 if key == "t" else -1.0,
            )

        def subtract(r):
            for u in range(2):
                tl = work.tile([P, 512], F32, name="diff", tag="diff", bufs=4)
                nc.vector.tensor_tensor(out=tl[:], in0=tanh_tiles[r, u, "t"][:], in1=tanh_tiles[r, u, "h"][:], op=ALU.add)
                tanh_tiles[r, u, "e"] = tl

        def sigmoid(r):
            g, dp = divmod(r, 4)
            sig[r] = work.tile([P, 4, 256], F32, name="sig", tag="sig", bufs=2)
            nc.scalar.activation(out=sig[r][:], in_=raw["a", g][:, :, 256 * dp : 256 * (dp + 1)], func=ACT.Sigmoid)

        def row_weight(r):
            g = r // 4
            weight[r] = work.tile([P, 4, 256], F32, name="weight", tag="weight", bufs=2)
            for s in range(4):
                if r in GP_ROUNDS:
                    nc.gpsimd.tensor_scalar(
                        out=weight[r][:, s, :],
                        in0=sig[r][:, s, :],
                        scalar1=c_bf[:, g, s : s + 1],
                        scalar2=0.0,
                        op0=ALU.mult,
                        op1=ALU.add,
                    )
                    continue
                nc.vector.tensor_scalar(
                    out=weight[r][:, s, :], in0=sig[r][:, s, :], scalar1=c_bf[:, g, s : s + 1], scalar2=None, op0=ALU.mult
                )

        def back(r, units=(0, 1)):
            for u in units:
                ps = psum.tile([P, 4, P], F32, name="e_ps", tag="m", bufs=4)
                e_ps[r, u] = ps
                for s in range(4):
                    parts = ["e"] if (r, u, "e") in tanh_tiles else ["t", "h"]
                    for key in parts:
                        nc.tensor.matmul(
                            ps[:, s, :],
                            lhsT=tanh_tiles[r, u, key][:, P * s : P * (s + 1)],
                            rhs=ident[:],
                            is_transpose=True,
                            start=(key == parts[0]),
                            stop=(key == parts[-1]),
                        )

        def error(r, units=(0, 1)):
            if 0 in units:
                q_in[r] = work.tile([P, 256, 4], BF16, name="q_in", tag="q_in", align_bytes=64)
            for u in units:
                nc.vector.tensor_tensor(
                    out=q_in[r][:, P * u : P * (u + 1), :],
                    in0=e_ps[r, u][:].rearrange("p s d -> p d s"),
                    in1=weight[r][:, :, P * u : P * (u + 1)].rearrange("p s d -> p d s"),
                    op=ALU.mult,
                )

        def quantise_q(r):
            q_codes[r] = keep("q_codes%d" % r, [P, 256], U32)
            q_scales[r] = keep("q_scales%d" % r, [P, 256], U8)
            nc.vector.quantize_mx(
                out=q_codes[r][:].bitcast(FP8X4),
                scales=q_scales[r][:],
                in_=q_in[r][:].rearrange("p d s -> p (d s)"),
            )

        out_view = out.rearrange("(e p) d -> p e d", p=P)

        def final(j, hf):
            width = 1 if j == 3 else 2
            for n in range(4 // width):
                ps = psum.tile([P, width, 256], F32, name="o_ps", tag="m", bufs=4)
                for i in range(width):
                    el = width * n + i
                    for g in range(2):
                        nc.tensor.matmul_mx(
                            out=ps[:, i, :],
                            lhsT=x_codes[g, hf][:, P * el : P * (el + 1)].bitcast(FP8X4),
                            lhsT_scale=x_scales[g, hf][:, P * el : P * (el + 1)],
                            rhs=q_codes[4 * g + j][:].bitcast(FP8X4),
                            rhs_scale=q_scales[4 * g + j][:],
                            start=(g == 0),
                            stop=(g == 1),
                        )
                res = work.tile([P, width, 256], F32, name="res", tag="res%d" % width, bufs=8 if width == 1 else 12)
                if n % 2 == 0:
                    nc.scalar.activation(out=res[:], in_=ps[:], func=ACT.Copy, scale=1.0 / 32.0)
                else:
                    nc.vector.tensor_scalar(out=res[:], in0=ps[:], scalar1=1.0 / 32.0, scalar2=None, op0=ALU.mult)
                e0 = 4 * hf + width * n
                nc.sync.dma_start(out=out_view[:, e0 : e0 + width, 256 * j : 256 * (j + 1)], in_=res[:])

        warm_pe(6, 512)
        for s in range(4):
            turn_slot("t", 0, s, "z", "ssss"[s])
            if s in (1, 3):
                warm_pe(1, 512)
        for s in range(4):
            if s == 0 and 0 > 0:
                if s == 0:
                    quantise_th("t", 0, 0)
                    quantise_th("t", 0, 1)
                for k in range(0):
                    forward(k // 2, k % 2, "t")
            turn_slot("h", 0, s, "m", "ssss"[s])
            if s == 3:
                small_vectors()
            if s in (0, 2):
                warm_pe(1, 512, "z")
            if s == 1:
                quantise_th("t", 0, 0)
            if s == 3:
                quantise_th("t", 0, 1)
        quantise_th("h", 0, 0)
        quantise_th("h", 0, 1)
        do_x(6)
        late = [(key, s) for key in ("t", "h") for s in range(4)]
        mid = {2:(2,4),3:(6,8)}
        end = {1:(0,2),2:(4,6)}
        xa = {1:1,2:2,3:0,4:0,5:0,6:2}
        xb = {1:3,2:1,3:2,4:3,5:1,6:3}
        for step in range(10):
            if step == 3:
                quantise_th("t", 1, 0)
                quantise_th("t", 1, 1)
            if 1 <= step <= 8:
                row_weight(step - 1)
            if step < 8:
                for key in ("t", "h"):
                    for u in range(2):
                        forward(step, u, key)
                    if key == "t":
                        if step in (99,):
                            do_x(xa.get(step, 0))
                            back(step - 1)
                            error(step - 1)
                        for i, (k2, s) in enumerate(late[slice(*mid.get(step, (0, 0)))]):
                            turn_slot(k2, 1, s, "m", "vvss"[s])
                            if k2 == "h" and s == 3:
                                quantise_th("h", 1, 0)
                                quantise_th("h", 1, 1)
                sigmoid(step)
            if 1 <= step <= 8 and step not in (99,):
                do_x(xa.get(step, 0))
                back(step - 1)
                error(step - 1)
            for i, (k2, s) in enumerate(late[slice(*end.get(step, (0, 0)))]):
                turn_slot(k2, 1, s, "m", "vvss"[s])
                if k2 == "h" and s == 3:
                    quantise_th("h", 1, 0)
                    quantise_th("h", 1, 1)
            if 1 <= step <= 8:
                quantise_q(step - 1)
                if step in ():
                    subtract(step)
                do_x(xb.get(step, 0))
            for j, hf in {6: [(0, 0)], 7: [(0, 1), (1, 0)], 8: [(1, 1), (2, 0), (2, 1)], 9: [(3, 0), (3, 1)]}.get(step, ()):
                final(j, hf)
